import numpy as np
import ml_dtypes


def mxq(x, axis, fmt="e4m3"):
    dtype, down = {"e4m3": (ml_dtypes.float8_e4m3fn, 7), "e5m2": (ml_dtypes.float8_e5m2, 14)}[fmt]
    v = np.moveaxis(np.asarray(x, np.float32).astype(ml_dtypes.bfloat16).astype(np.float64), axis, -1)
    blocks = v.reshape(v.shape[:-1] + (-1, 32))
    amax = np.abs(blocks).max(-1, keepdims=True)
    byte = np.maximum(np.where(amax > 0, np.frexp(amax)[1] - 1 + 127, 0) - down, 1)
    scale = np.exp2(byte - 127.0)
    codes = (blocks / scale).astype(np.float32).astype(dtype).astype(np.float64)
    return np.moveaxis((codes * scale).reshape(v.shape), -1, axis)


WIDE = False


def mx_kscale(k):
    if not WIDE:
        return np.ones(k)
    levels = np.array([10, -10, 5, -5, 0])
    if k % 512:
        return np.exp2(np.random.permutation(np.resize(levels, k // 32))).repeat(32)
    a = np.empty((k // 512, 16))
    for p in range(k // 512):
        a[p, :8] = np.random.permutation(np.resize(levels, 8))
        for g in range(8):
            far = levels[np.abs(levels - a[p, g]) >= 10]
            a[p, g + 8] = far[np.random.randint(len(far))]
    return np.exp2(a.ravel()).repeat(32)


def f64(x):
    return np.asarray(x).astype(np.float64)


def striped(idx):
    return np.tile(idx.reshape(-1, 16).T, (8, 1)).astype(np.uint16)


def unstriped(offs):
    return offs[:16].T.reshape(-1).astype(np.int64)


def pack_weight(w):
    k, n = w.shape
    w = f64(np.asarray(w, np.float32).astype(ml_dtypes.bfloat16)).reshape(k // 32, 32, n)
    amax = np.abs(w).max(1)
    byte = np.clip(np.where(amax > 0, np.frexp(amax)[1] - 1 + 127 - 7, 1), 1, 254)
    scaled = (w * np.exp2(127.0 - byte)[:, None, :]).reshape(k, n).astype(np.float32)
    words = np.ascontiguousarray(scaled.reshape(k // 512, 128, 4, n).transpose(0, 1, 3, 2)).astype(ml_dtypes.float8_e4m3fn).view(np.uint8)
    return words, np.ascontiguousarray(byte.astype(np.uint8).reshape(k // 512, 16, n))


def unpack_weight(words, scales):
    g, p, n, _ = words.shape
    vals = np.ascontiguousarray(words).view(ml_dtypes.float8_e4m3fn).astype(np.float64) * np.repeat(np.exp2(scales.astype(np.float64) - 127.0), 8, axis=1)[..., None]
    return vals.transpose(0, 1, 3, 2).reshape(g * 512, n)


K, T, S, N, H, W, U = 512, 2048, 512, 128, 512, 1024, 1024


def setup_inputs():
    n = np.random.standard_normal
    s = mx_kscale(K)[:, None]
    u = mx_kscale(H)
    packed_xT = pack_weight(n((K, T)) * s)
    packed_eT = pack_weight(n((K, W)) * s)
    return {
        "x_words": packed_xT[0],
        "x_scales": packed_xT[1],
        "w1": (n((K, H)) / np.sqrt(K) / s).astype(np.float32),
        "e_words": packed_eT[0],
        "e_scales": packed_eT[1],
        "w2": (n((K, H)) / np.sqrt(K) / s).astype(np.float32),
        "unit": (np.random.uniform(0.6, 1.4, (H, 1)) * u[:, None]).astype(np.float32),
        "w3": (n((H, N)) / np.sqrt(H) / u[:, None]).astype(np.float32),
        "offs": striped(np.random.permutation(T)[:S]),
        "wrd": striped(np.random.permutation(W)[:S]),
        "t1": striped(np.random.permutation(np.concatenate([np.arange(S), np.random.randint(0, S, U - S)]))),
        "t2": striped(np.random.permutation(np.concatenate([np.arange(S), np.random.randint(0, S, U - S)]))),
        "qw": striped(np.random.permutation(np.concatenate([np.arange(S), np.random.randint(0, S, U - S)]))),
    }


def reference(x_words, x_scales, w1, e_words, e_scales, w2, unit, w3, offs, wrd, t1, t2, qw):
    xq = unpack_weight(x_words, x_scales)[:, unstriped(offs)]
    y = mxq(f64(w1), 0, "e4m3").T @ xq
    y_1 = y[:, unstriped(t1)]
    y_2 = y[:, unstriped(t2)]
    mot = y_1 - y_2
    e_wrd = unpack_weight(e_words, e_scales)[:, unstriped(wrd)]
    ye = mxq(f64(w2), 0, "e4m3").T @ e_wrd
    eq_ = ye[:, unstriped(qw)]
    hid = f64(unit) * (mot * eq_)
    return mxq(f64(w3), 0, "e4m3").T @ mxq(hid, 0, "e4m3")

@@ -1,0 +1,198 @@
+from contextlib import ExitStack
+
+import concourse.mybir as mybir
+
+K, T, S, N, H, W, U = 512, 2048, 512, 128, 512, 1024, 1024
+FLOPS = 2 * (K * H * S * 2 + H * N * U)
+
+F32 = mybir.dt.float32
+BF16 = mybir.dt.bfloat16
+I32 = mybir.dt.int32
+U32 = mybir.dt.uint32
+U16 = mybir.dt.uint16
+U8 = mybir.dt.uint8
+FP8X4 = mybir.dt.float8_e4m3fn_x4
+COPY = mybir.ActivationFunctionType.Copy
+MULT = mybir.AluOpType.mult
+SUB = mybir.AluOpType.subtract
+
+P = 128
+PACK = 4
+CHUNK = 256
+CHUNKS = U // CHUNK
+LIST_COLS = CHUNK // 16
+SCALAR_CAST_COLS = 44
+T2_ON_VECTOR = {0: (), 1: (), 2: (), 3: ()}
+T1_ON_SCALAR = {0: (), 1: (), 2: (), 3: (1, 2, 3)}
+
+
+def tile_picked_yvideoq_mot_p_kernel(
+    tc, x_words, x_scales, w1, e_words, e_scales, w2, unit, w3, offs, wrd, t1, t2, qw, out
+):
+    nc = tc.nc
+    with ExitStack() as ctx:
+        keep = ctx.enter_context(tc.tile_pool(name="keep", bufs=1))
+        psum = ctx.enter_context(tc.psum_pool(name="psum", bufs=1))
+
+        def load_list(name, src):
+            tile = keep.tile(list(src.shape), U16, name=name)
+            nc.sync.dma_start(tile[:], src)
+            return tile
+
+        def load_words(name, src, width):
+            tile = keep.tile([P, width], U32, name=name, align_bytes=64)
+            nc.sync.dma_start(tile[:].bitcast(I32), src[0].rearrange("p n t -> p (n t)").bitcast(I32))
+            return tile
+
+        def load_scales(name, src, width, clear, queue):
+            tile = keep.tile([P, width], U8, name=name, align_bytes=64)
+            clear.memset(tile[:].bitcast(I32), 0)
+            for q in range(4):
+                queue.dma_start(tile[32 * q : 32 * q + 4, :].bitcast(I32), src[0, 4 * q : 4 * q + 4, :].bitcast(I32))
+            return tile
+
+        def load_weight(name, src, width):
+            tile = keep.tile([P, PACK, width], F32, name=name)
+            nc.sync.dma_start(tile[:], src.rearrange("(p j) c -> p j c", j=PACK))
+            return tile
+
+        e_table = load_words("e_table", e_words, W)
+        e_bytes = load_scales("e_bytes", e_scales, W, nc.gpsimd, nc.sync)
+        wrd_sb = load_list("wrd_sb", wrd)
+        w2_raw = load_weight("w2_raw", w2, H)
+        offs_sb = load_list("offs_sb", offs)
+        x_table = load_words("x_table", x_words, T)
+        unit_sb = keep.tile([P, PACK], F32, name="unit_sb")
+        nc.sync.dma_start(unit_sb[:], unit.rearrange("(p t) o -> p (t o)", t=PACK))
+        qw_sb = load_list("qw_sb", qw)
+        x_bytes = load_scales("x_bytes", x_scales, T, nc.gpsimd, nc.sync)
+        w1_raw = load_weight("w1_raw", w1, H)
+        t2_sb = load_list("t2_sb", t2)
+        t1_sb = load_list("t1_sb", t1)
+        w3_raw = load_weight("w3_raw", w3, N)
+
+        ye = [keep.tile([P, S], F32, name="ye%d" % t) for t in range(PACK)]
+        y = [keep.tile([P, S], F32, name="y%d" % t) for t in range(PACK)]
+
+        def dealt_views(name, raw):
+            grouped = keep.tile([P, PACK * H], BF16, name=name, tag=name, align_bytes=64)
+            dst = grouped[:].rearrange("p (t m j) -> p m j t", t=PACK, j=PACK)
+            src = raw[:].rearrange("p j (m t) -> p m j t", t=PACK)
+            return grouped, dst, src
+
+        def first_product(name, grouped, picked_words, picked_bytes, first_bank):
+            codes = keep.tile([P, H], U32, name=name + "_codes", align_bytes=64)
+            scales = keep.tile([P, H], U8, name=name + "_scales", align_bytes=64)
+            banks = []
+            for t in range(PACK):
+                cols = slice(t * P, (t + 1) * P)
+                nc.vector.quantize_mx(
+                    out=codes[:, cols].bitcast(FP8X4),
+                    scales=scales[:, cols],
+                    in_=grouped[:, t * PACK * P : (t + 1) * PACK * P],
+                )
+                bank = psum.tile([P, S], F32, name=name + "_acc%d" % t, tag="bank%d" % (first_bank + t))
+                nc.tensor.matmul_mx(
+                    out=bank[:],
+                    lhsT=codes[:, cols].bitcast(FP8X4),
+                    lhsT_scale=scales[:, cols],
+                    rhs=picked_words[:].bitcast(FP8X4),
+                    rhs_scale=picked_bytes[:],
+                    start=True,
+                    stop=True,
+                )
+                banks.append(bank)
+            return banks
+
+        e_picked = keep.tile([P, S], U32, name="e_picked", align_bytes=64)
+        e_picked_bytes = keep.tile([P, S], U8, name="e_picked_bytes", align_bytes=64)
+        w2_grouped, dst, src = dealt_views("w2_grouped", w2_raw)
+        nc.vector.tensor_copy(e_picked[:], e_table[:].indirect(wrd_sb[:]))
+        nc.vector.tensor_copy(e_picked_bytes[:], e_bytes[:].indirect(wrd_sb[:]))
+        nc.scalar.activation(dst[:, :SCALAR_CAST_COLS], src[:, :SCALAR_CAST_COLS], COPY)
+        nc.vector.tensor_copy(dst[:, SCALAR_CAST_COLS:], src[:, SCALAR_CAST_COLS:])
+        ye_banks = first_product("w2", w2_grouped, e_picked, e_picked_bytes, 0)
+
+        def entries_of(c):
+            return slice(c * LIST_COLS, (c + 1) * LIST_COLS)
+
+        def gather_eq(c, t):
+            nc.scalar.activation(eq[c][:, t, :], ye[t][:].indirect(qw_sb[:, entries_of(c)]), COPY)
+
+        eq = [keep.tile([P, PACK, CHUNK], F32, name="eq%d" % c, tag="eq", bufs=2) for c in range(2)]
+        for t in range(PACK):
+            nc.scalar.activation(ye[t][:], ye_banks[t][:], COPY, scale=unit_sb[:, t : t + 1])
+            gather_eq(0, t)
+            gather_eq(1, t)
+
+        x_picked = keep.tile([P, S], U32, name="x_picked", tag="w2_grouped", align_bytes=64)
+        x_picked_bytes = keep.tile([P, S], U8, name="x_picked_bytes", align_bytes=64)
+        w1_grouped, dst, src = dealt_views("w1_grouped", w1_raw)
+        nc.vector.tensor_copy(x_picked[:], x_table[:].indirect(offs_sb[:]))
+        nc.vector.tensor_copy(dst, src)
+        nc.vector.tensor_copy(x_picked_bytes[:], x_bytes[:].indirect(offs_sb[:]))
+        y_banks = first_product("w1", w1_grouped, x_picked, x_picked_bytes, PACK)
+
+        w3_grouped = keep.tile([P, PACK * N], BF16, name="w3_grouped", align_bytes=64)
+        w3_codes = keep.tile([P, N], U32, name="w3_codes", align_bytes=64)
+        w3_scale = keep.tile([P, N], U8, name="w3_scale", align_bytes=64)
+        nc.vector.tensor_copy(
+            w3_grouped[:].rearrange("p (c i j) -> p c j i", i=4, j=PACK),
+            w3_raw[:].rearrange("p j (c i) -> p c j i", i=4),
+        )
+        nc.vector.tensor_copy(y[0][:], y_banks[0][:])
+        nc.vector.quantize_mx(out=w3_codes[:].bitcast(FP8X4), scales=w3_scale[:], in_=w3_grouped[:])
+        for t in range(1, PACK):
+            nc.vector.tensor_copy(y[t][:], y_banks[t][:])
+
+        for c in range(CHUNKS):
+            entries = entries_of(c)
+            cols = slice(c * CHUNK, (c + 1) * CHUNK)
+            y2 = keep.tile([P, PACK, CHUNK], F32, name="y2_%d" % c)
+            mot = keep.tile([P, PACK, CHUNK], F32, name="mot%d" % c)
+            for t in range(PACK):
+                window = y[t][:].indirect(t2_sb[:, entries])
+                if t in T2_ON_VECTOR[c]:
+                    nc.vector.tensor_copy(y2[:, t, :], window)
+                else:
+                    nc.scalar.activation(y2[:, t, :], window, COPY)
+            plain = T1_ON_SCALAR[c]
+            if plain:
+                y1 = keep.tile([P, PACK, CHUNK], F32, name="y1_%d" % c)
+            for t in range(PACK):
+                window = y[t][:].indirect(t1_sb[:, entries])
+                if t in plain:
+                    nc.scalar.activation(y1[:, t, :], window, COPY)
+                else:
+                    nc.vector.tensor_tensor(mot[:, t, :], window, y2[:, t, :], SUB)
+            if plain:
+                planes = slice(plain[0], plain[-1] + 1)
+                nc.vector.tensor_tensor(mot[:, planes, :], y1[:, planes, :], y2[:, planes, :], SUB)
+
+            hid = keep.tile([P, CHUNK * PACK], BF16, name="hid%d" % c, align_bytes=64)
+            nc.vector.tensor_tensor(
+                hid[:].rearrange("p (c i t) -> p c t i", i=4, t=PACK),
+                mot[:].rearrange("p t (c i) -> p c t i", i=4),
+                eq[c][:].rearrange("p t (c i) -> p c t i", i=4),
+                MULT,
+            )
+            if c + 2 < CHUNKS:
+                eq.append(keep.tile([P, PACK, CHUNK], F32, name="eq%d" % (c + 2), tag="eq", bufs=2))
+                for t in range(PACK):
+                    gather_eq(c + 2, t)
+            hid_codes = keep.tile([P, CHUNK], U32, name="hid_codes%d" % c, align_bytes=64)
+            hid_scale = keep.tile([P, CHUNK], U8, name="hid_scale%d" % c, align_bytes=64)
+            nc.vector.quantize_mx(out=hid_codes[:].bitcast(FP8X4), scales=hid_scale[:], in_=hid[:])
+            acc = psum.tile([P, CHUNK], F32, name="acc%d" % c, tag="bank%d" % c)
+            nc.tensor.matmul_mx(
+                out=acc[:],
+                lhsT=w3_codes[:].bitcast(FP8X4),
+                lhsT_scale=w3_scale[:],
+                rhs=hid_codes[:].bitcast(FP8X4),
+                rhs_scale=hid_scale[:],
+                start=True,
+                stop=True,
+            )
+            result = keep.tile([P, CHUNK], F32, name="result%d" % c)
+            nc.scalar.activation(result[:], acc[:], COPY)
+            nc.sync.dma_start(out[:, cols], result[:])

@@ -14,16 +14,15 @@ U8 = mybir.dt.uint8
 FP8X4 = mybir.dt.float8_e4m3fn_x4
 COPY = mybir.ActivationFunctionType.Copy
 MULT = mybir.AluOpType.mult
+ADD = mybir.AluOpType.add
 SUB = mybir.AluOpType.subtract
 
 P = 128
 PACK = 4
-CHUNK = 256
-CHUNKS = U // CHUNK
-LIST_COLS = CHUNK // 16
-SCALAR_CAST_COLS = 44
-T2_ON_VECTOR = {0: (), 1: (), 2: (), 3: ()}
-T1_ON_SCALAR = {0: (), 1: (), 2: (), 3: (1, 2, 3)}
+HALF = U // 2
+WINDOW = S + 16
+W2_SCALAR_COLS = 20
+TAIL_PIECES = (256, 128, 128)
 
 
 def tile_picked_yvideoq_mot_p_kernel(
@@ -44,53 +43,60 @@ def tile_picked_yvideoq_mot_p_kernel(
             nc.sync.dma_start(tile[:].bitcast(I32), src[0].rearrange("p n t -> p (n t)").bitcast(I32))
             return tile
 
-        def load_scales(name, src, width, clear, queue):
+        def load_scales(name, src, width, queue):
             tile = keep.tile([P, width], U8, name=name, align_bytes=64)
-            clear.memset(tile[:].bitcast(I32), 0)
+            nc.gpsimd.memset(tile[:].bitcast(I32), 0)
             for q in range(4):
-                queue.dma_start(tile[32 * q : 32 * q + 4, :].bitcast(I32), src[0, 4 * q : 4 * q + 4, :].bitcast(I32))
+                queue.dma_start(
+                    tile[32 * q : 32 * q + 4, :].bitcast(I32), src[0, 4 * q : 4 * q + 4, :].bitcast(I32)
+                )
             return tile
 
-        def load_weight(name, src, width):
-            tile = keep.tile([P, PACK, width], F32, name=name)
+        def load_weight(name, src):
+            tile = keep.tile([P, PACK, src.shape[1]], F32, name=name, tag=name, align_bytes=64)
             nc.sync.dma_start(tile[:], src.rearrange("(p j) c -> p j c", j=PACK))
             return tile
 
         e_table = load_words("e_table", e_words, W)
-        e_bytes = load_scales("e_bytes", e_scales, W, nc.gpsimd, nc.sync)
+        e_bytes = load_scales("e_bytes", e_scales, W, nc.sync)
         wrd_sb = load_list("wrd_sb", wrd)
-        w2_raw = load_weight("w2_raw", w2, H)
-        offs_sb = load_list("offs_sb", offs)
+        w2_low = load_weight("w2_low", w2[:, : H // 2])
+        w2_high = load_weight("w2_high", w2[:, H // 2 :])
+        qw_sb = load_list("qw_sb", qw)
         x_table = load_words("x_table", x_words, T)
+        offs_sb = load_list("offs_sb", offs)
+        x_bytes = load_scales("x_bytes", x_scales, T, nc.sync)
+        w1_low = load_weight("w1_low", w1[:, : H // 2])
+        w1_high = load_weight("w1_high", w1[:, H // 2 :])
         unit_sb = keep.tile([P, PACK], F32, name="unit_sb")
         nc.sync.dma_start(unit_sb[:], unit.rearrange("(p t) o -> p (t o)", t=PACK))
-        qw_sb = load_list("qw_sb", qw)
-        x_bytes = load_scales("x_bytes", x_scales, T, nc.gpsimd, nc.sync)
-        w1_raw = load_weight("w1_raw", w1, H)
         t2_sb = load_list("t2_sb", t2)
         t1_sb = load_list("t1_sb", t1)
-        w3_raw = load_weight("w3_raw", w3, N)
+        w3_raw = load_weight("w3_raw", w3)
 
-        ye = [keep.tile([P, S], F32, name="ye%d" % t) for t in range(PACK)]
-        y = [keep.tile([P, S], F32, name="y%d" % t) for t in range(PACK)]
+        def window_tile(name, tag, width=WINDOW):
+            tile = keep.tile([P, width], F32, name=name, tag=tag, align_bytes=64)
+            nc.gpsimd.memset(tile[:, S:], 0.0)
+            return tile
 
-        def dealt_views(name, raw):
-            grouped = keep.tile([P, PACK * H], BF16, name=name, tag=name, align_bytes=64)
-            dst = grouped[:].rearrange("p (t m j) -> p m j t", t=PACK, j=PACK)
-            src = raw[:].rearrange("p j (m t) -> p m j t", t=PACK)
-            return grouped, dst, src
+        def dealt(grouped):
+            return grouped[:].rearrange("p (t m j) -> p m j t", t=PACK, j=PACK)
+
+        def by_plane(raw):
+            return raw[:].rearrange("p j (m t) -> p m j t", t=PACK)
 
         def first_product(name, grouped, picked_words, picked_bytes, first_bank):
             codes = keep.tile([P, H], U32, name=name + "_codes", align_bytes=64)
             scales = keep.tile([P, H], U8, name=name + "_scales", align_bytes=64)
+            for lo, hi in ((0, P), (P, H)):
+                nc.vector.quantize_mx(
+                    out=codes[:, lo:hi].bitcast(FP8X4),
+                    scales=scales[:, lo:hi],
+                    in_=grouped[:, PACK * lo : PACK * hi],
+                )
             banks = []
             for t in range(PACK):
                 cols = slice(t * P, (t + 1) * P)
-                nc.vector.quantize_mx(
-                    out=codes[:, cols].bitcast(FP8X4),
-                    scales=scales[:, cols],
-                    in_=grouped[:, t * PACK * P : (t + 1) * PACK * P],
-                )
                 bank = psum.tile([P, S], F32, name=name + "_acc%d" % t, tag="bank%d" % (first_bank + t))
                 nc.tensor.matmul_mx(
                     out=bank[:],
@@ -104,35 +110,39 @@ def tile_picked_yvideoq_mot_p_kernel(
                 banks.append(bank)
             return banks
 
+        def entries(lst, first, count):
+            return lst[:, first // 16 : (first + count) // 16]
+
         e_picked = keep.tile([P, S], U32, name="e_picked", align_bytes=64)
         e_picked_bytes = keep.tile([P, S], U8, name="e_picked_bytes", align_bytes=64)
-        w2_grouped, dst, src = dealt_views("w2_grouped", w2_raw)
+        w2_grouped = keep.tile([P, PACK * H], BF16, name="w2_grouped", tag="handed_on", align_bytes=64)
         nc.vector.tensor_copy(e_picked[:], e_table[:].indirect(wrd_sb[:]))
         nc.vector.tensor_copy(e_picked_bytes[:], e_bytes[:].indirect(wrd_sb[:]))
-        nc.scalar.activation(dst[:, :SCALAR_CAST_COLS], src[:, :SCALAR_CAST_COLS], COPY)
-        nc.vector.tensor_copy(dst[:, SCALAR_CAST_COLS:], src[:, SCALAR_CAST_COLS:])
+        mid = P // 2
+        cut = mid + W2_SCALAR_COLS
+        nc.scalar.activation(dealt(w2_grouped)[:, :mid], by_plane(w2_low), COPY)
+        nc.scalar.activation(dealt(w2_grouped)[:, mid:cut], by_plane(w2_high)[:, :W2_SCALAR_COLS], COPY)
+        nc.vector.tensor_copy(dealt(w2_grouped)[:, cut:], by_plane(w2_high)[:, W2_SCALAR_COLS:])
         ye_banks = first_product("w2", w2_grouped, e_picked, e_picked_bytes, 0)
 
-        def entries_of(c):
-            return slice(c * LIST_COLS, (c + 1) * LIST_COLS)
+        eq_a = keep.tile([P, PACK * HALF], F32, name="eq_a", tag="eq")
+        ye = []
 
-        def gather_eq(c, t):
-            nc.scalar.activation(eq[c][:, t, :], ye[t][:].indirect(qw_sb[:, entries_of(c)]), COPY)
+        def gather_eq(dst, t, first, count):
+            nc.scalar.activation(dst, ye[t][:].indirect(entries(qw_sb, first, count)), COPY)
 
-        eq = [keep.tile([P, PACK, CHUNK], F32, name="eq%d" % c, tag="eq", bufs=2) for c in range(2)]
-        for t in range(PACK):
-            nc.scalar.activation(ye[t][:], ye_banks[t][:], COPY, scale=unit_sb[:, t : t + 1])
-            gather_eq(0, t)
-            gather_eq(1, t)
+        for t in range(PACK - 1):
+            ye.append(window_tile("ye%d" % t, "ye%d" % t))
+            nc.scalar.activation(ye[t][:, :S], ye_banks[t][:], COPY)
+            gather_eq(eq_a[:, t * HALF : (t + 1) * HALF], t, 0, HALF)
 
-        x_picked = keep.tile([P, S], U32, name="x_picked", tag="w2_grouped", align_bytes=64)
-        x_picked_bytes = keep.tile([P, S], U8, name="x_picked_bytes", align_bytes=64)
-        w1_grouped, dst, src = dealt_views("w1_grouped", w1_raw)
+        x_picked = keep.tile([P, S], U32, name="x_picked", tag="handed_on", align_bytes=64)
+        x_picked_bytes = keep.tile([P, S], U8, name="x_picked_bytes", tag="w2_high", align_bytes=64)
+        w1_grouped = keep.tile([P, PACK * H], BF16, name="w1_grouped", align_bytes=64)
         nc.vector.tensor_copy(x_picked[:], x_table[:].indirect(offs_sb[:]))
-        nc.vector.tensor_copy(dst, src)
         nc.vector.tensor_copy(x_picked_bytes[:], x_bytes[:].indirect(offs_sb[:]))
-        y_banks = first_product("w1", w1_grouped, x_picked, x_picked_bytes, PACK)
-
+        nc.vector.tensor_copy(dealt(w1_grouped)[:, :mid], by_plane(w1_low))
+        nc.vector.tensor_copy(dealt(w1_grouped)[:, mid:], by_plane(w1_high))
         w3_grouped = keep.tile([P, PACK * N], BF16, name="w3_grouped", align_bytes=64)
         w3_codes = keep.tile([P, N], U32, name="w3_codes", align_bytes=64)
         w3_scale = keep.tile([P, N], U8, name="w3_scale", align_bytes=64)
@@ -140,59 +150,81 @@ def tile_picked_yvideoq_mot_p_kernel(
             w3_grouped[:].rearrange("p (c i j) -> p c j i", i=4, j=PACK),
             w3_raw[:].rearrange("p j (c i) -> p c j i", i=4),
         )
-        nc.vector.tensor_copy(y[0][:], y_banks[0][:])
-        nc.vector.quantize_mx(out=w3_codes[:].bitcast(FP8X4), scales=w3_scale[:], in_=w3_grouped[:])
-        for t in range(1, PACK):
-            nc.vector.tensor_copy(y[t][:], y_banks[t][:])
+        y_banks = first_product("w1", w1_grouped, x_picked, x_picked_bytes, PACK)
+        y = [window_tile("y%d" % t, "y%d" % t, 2 * S if t == 0 else WINDOW) for t in range(PACK)]
+        neg_y2 = [keep.tile([P, PACK, HALF], F32, name="neg_y2_%d" % h) for h in range(2)]
+        mot = [keep.tile([P, PACK, HALF], F32, name="mot%d" % h) for h in range(2)]
 
-        for c in range(CHUNKS):
-            entries = entries_of(c)
-            cols = slice(c * CHUNK, (c + 1) * CHUNK)
-            y2 = keep.tile([P, PACK, CHUNK], F32, name="y2_%d" % c)
-            mot = keep.tile([P, PACK, CHUNK], F32, name="mot%d" % c)
-            for t in range(PACK):
-                window = y[t][:].indirect(t2_sb[:, entries])
-                if t in T2_ON_VECTOR[c]:
-                    nc.vector.tensor_copy(y2[:, t, :], window)
-                else:
-                    nc.scalar.activation(y2[:, t, :], window, COPY)
-            plain = T1_ON_SCALAR[c]
-            if plain:
-                y1 = keep.tile([P, PACK, CHUNK], F32, name="y1_%d" % c)
-            for t in range(PACK):
-                window = y[t][:].indirect(t1_sb[:, entries])
-                if t in plain:
-                    nc.scalar.activation(y1[:, t, :], window, COPY)
-                else:
-                    nc.vector.tensor_tensor(mot[:, t, :], window, y2[:, t, :], SUB)
-            if plain:
-                planes = slice(plain[0], plain[-1] + 1)
-                nc.vector.tensor_tensor(mot[:, planes, :], y1[:, planes, :], y2[:, planes, :], SUB)
+        def gather_y2(h, t):
+            window = y[t][:].indirect(entries(t2_sb, h * HALF, HALF))
+            nc.scalar.activation(neg_y2[h][:, t, :], window, COPY, scale=-1.0)
 
-            hid = keep.tile([P, CHUNK * PACK], BF16, name="hid%d" % c, align_bytes=64)
+        def motion(h, t, op=ADD):
+            window = y[t][:].indirect(entries(t1_sb, h * HALF, HALF))
+            nc.vector.tensor_tensor(mot[h][:, t, :], window, neg_y2[h][:, t, :], op)
+
+        for t in range(PACK):
+            gain = unit_sb[:, t : t + 1]
+            if t == 0:
+                nc.vector.tensor_scalar(y[t][:, :S], y_banks[t][:], gain, None, MULT)
+                nc.vector.quantize_mx(out=w3_codes[:].bitcast(FP8X4), scales=w3_scale[:], in_=w3_grouped[:])
+                nc.vector.tensor_copy(neg_y2[0][:, 0, :], y[0][:].indirect(entries(t2_sb, 0, HALF)))
+            else:
+                nc.scalar.activation(y[t][:, :S], y_banks[t][:], COPY, scale=gain)
+                gather_y2(0, t)
+
+        ye.append(window_tile("ye3", "handed_on"))
+        nc.scalar.activation(ye[3][:, :S], ye_banks[3][:], COPY)
+        gather_eq(eq_a[:, 3 * HALF :], 3, 0, HALF)
+
+        def multiply(name, mot_cols, eq_cols, width):
+            hid = keep.tile([P, width * PACK], BF16, name="hid_" + name, align_bytes=64)
             nc.vector.tensor_tensor(
                 hid[:].rearrange("p (c i t) -> p c t i", i=4, t=PACK),
-                mot[:].rearrange("p t (c i) -> p c t i", i=4),
-                eq[c][:].rearrange("p t (c i) -> p c t i", i=4),
+                mot_cols.rearrange("p t (c i) -> p c t i", i=4),
+                eq_cols.rearrange("p (t c i) -> p c t i", t=PACK, i=4),
                 MULT,
             )
-            if c + 2 < CHUNKS:
-                eq.append(keep.tile([P, PACK, CHUNK], F32, name="eq%d" % (c + 2), tag="eq", bufs=2))
-                for t in range(PACK):
-                    gather_eq(c + 2, t)
-            hid_codes = keep.tile([P, CHUNK], U32, name="hid_codes%d" % c, align_bytes=64)
-            hid_scale = keep.tile([P, CHUNK], U8, name="hid_scale%d" % c, align_bytes=64)
-            nc.vector.quantize_mx(out=hid_codes[:].bitcast(FP8X4), scales=hid_scale[:], in_=hid[:])
-            acc = psum.tile([P, CHUNK], F32, name="acc%d" % c, tag="bank%d" % c)
+            return hid
+
+        def answer(name, hid, first, width, bank):
+            codes = keep.tile([P, width], U32, name="hid_codes_" + name, align_bytes=64)
+            scales = keep.tile([P, width], U8, name="hid_scales_" + name, align_bytes=64)
+            nc.vector.quantize_mx(out=codes[:].bitcast(FP8X4), scales=scales[:], in_=hid[:])
+            acc = psum.tile([P, width], F32, name="acc_" + name, tag="bank%d" % bank)
             nc.tensor.matmul_mx(
                 out=acc[:],
                 lhsT=w3_codes[:].bitcast(FP8X4),
                 lhsT_scale=w3_scale[:],
-                rhs=hid_codes[:].bitcast(FP8X4),
-                rhs_scale=hid_scale[:],
+                rhs=codes[:].bitcast(FP8X4),
+                rhs_scale=scales[:],
                 start=True,
                 stop=True,
             )
-            result = keep.tile([P, CHUNK], F32, name="result%d" % c)
+            result = keep.tile([P, width], F32, name="result_" + name)
             nc.scalar.activation(result[:], acc[:], COPY)
-            nc.sync.dma_start(out[:, cols], result[:])
+            nc.sync.dma_start(out[:, first : first + width], result[:])
+
+        for t in range(PACK):
+            motion(0, t, SUB if t == 0 else ADD)
+        for t in range(PACK):
+            gather_y2(1, t)
+        hid_a = multiply("a", mot[0][:], eq_a[:], HALF)
+        motion(1, 0)
+        answer("a", hid_a, 0, HALF, 0)
+        for t in range(1, PACK):
+            motion(1, t)
+
+        eq_b = keep.tile([P, PACK * HALF], F32, name="eq_b", tag="eq")
+        waiting = None
+        first = 0
+        for k, width in enumerate(TAIL_PIECES):
+            piece = eq_b[:, PACK * first : PACK * (first + width)]
+            for t in range(PACK):
+                gather_eq(piece[:, t * width : (t + 1) * width], t, HALF + first, width)
+            hid = multiply("b%d" % k, mot[1][:, :, first : first + width], piece, width)
+            if waiting:
+                answer(*waiting)
+            waiting = ("b%d" % k, hid, HALF + first, width, 1 + k)
+            first = first + width
+        answer(*waiting)

@@ -22,6 +22,7 @@ PACK = 4
 HALF = U // 2
 WINDOW = S + 16
 W2_SCALAR_COLS = 20
+X_SCALE_ROW = 4
 TAIL_PIECES = (256, 128, 128)
 
 
@@ -43,13 +44,12 @@ def tile_picked_yvideoq_mot_p_kernel(
             nc.sync.dma_start(tile[:].bitcast(I32), src[0].rearrange("p n t -> p (n t)").bitcast(I32))
             return tile
 
-        def load_scales(name, src, width, queue):
+        def load_scales(name, src, width, row):
             tile = keep.tile([P, width], U8, name=name, align_bytes=64)
             nc.gpsimd.memset(tile[:].bitcast(I32), 0)
-            for q in range(4):
-                queue.dma_start(
-                    tile[32 * q : 32 * q + 4, :].bitcast(I32), src[0, 4 * q : 4 * q + 4, :].bitcast(I32)
-                )
+            rows = src[0].rearrange("(q r) n -> r q n", r=4)
+            for r in range(4):
+                nc.sync.dma_start(tile[row + r : P : 32, :].bitcast(I32), rows[r].bitcast(I32))
             return tile
 
         def load_weight(name, src):
@@ -58,14 +58,14 @@ def tile_picked_yvideoq_mot_p_kernel(
             return tile
 
         e_table = load_words("e_table", e_words, W)
-        e_bytes = load_scales("e_bytes", e_scales, W, nc.sync)
+        e_bytes = load_scales("e_bytes", e_scales, W, 0)
         wrd_sb = load_list("wrd_sb", wrd)
         w2_low = load_weight("w2_low", w2[:, : H // 2])
         w2_high = load_weight("w2_high", w2[:, H // 2 :])
         qw_sb = load_list("qw_sb", qw)
         x_table = load_words("x_table", x_words, T)
         offs_sb = load_list("offs_sb", offs)
-        x_bytes = load_scales("x_bytes", x_scales, T, nc.sync)
+        x_bytes = load_scales("x_bytes", x_scales, T, X_SCALE_ROW)
         w1_low = load_weight("w1_low", w1[:, : H // 2])
         w1_high = load_weight("w1_high", w1[:, H // 2 :])
         unit_sb = keep.tile([P, PACK], F32, name="unit_sb")
@@ -103,7 +103,7 @@ def tile_picked_yvideoq_mot_p_kernel(
                     lhsT=codes[:, cols].bitcast(FP8X4),
                     lhsT_scale=scales[:, cols],
                     rhs=picked_words[:].bitcast(FP8X4),
-                    rhs_scale=picked_bytes[:],
+                    rhs_scale=picked_bytes,
                     start=True,
                     stop=True,
                 )
@@ -123,7 +123,7 @@ def tile_picked_yvideoq_mot_p_kernel(
         nc.scalar.activation(dealt(w2_grouped)[:, :mid], by_plane(w2_low), COPY)
         nc.scalar.activation(dealt(w2_grouped)[:, mid:cut], by_plane(w2_high)[:, :W2_SCALAR_COLS], COPY)
         nc.vector.tensor_copy(dealt(w2_grouped)[:, cut:], by_plane(w2_high)[:, W2_SCALAR_COLS:])
-        ye_banks = first_product("w2", w2_grouped, e_picked, e_picked_bytes, 0)
+        ye_banks = first_product("w2", w2_grouped, e_picked, e_picked_bytes[:], 0)
 
         eq_a = keep.tile([P, PACK * HALF], F32, name="eq_a", tag="eq")
         ye = []
@@ -131,7 +131,7 @@ def tile_picked_yvideoq_mot_p_kernel(
         def gather_eq(dst, t, first, count):
             nc.scalar.activation(dst, ye[t][:].indirect(entries(qw_sb, first, count)), COPY)
 
-        for t in range(PACK - 1):
+        for t in range(PACK):
             ye.append(window_tile("ye%d" % t, "ye%d" % t))
             nc.scalar.activation(ye[t][:, :S], ye_banks[t][:], COPY)
             gather_eq(eq_a[:, t * HALF : (t + 1) * HALF], t, 0, HALF)
@@ -150,9 +150,12 @@ def tile_picked_yvideoq_mot_p_kernel(
             w3_grouped[:].rearrange("p (c i j) -> p c j i", i=4, j=PACK),
             w3_raw[:].rearrange("p j (c i) -> p c j i", i=4),
         )
-        y_banks = first_product("w1", w1_grouped, x_picked, x_picked_bytes, PACK)
+        y_banks = first_product("w1", w1_grouped, x_picked, x_picked_bytes[X_SCALE_ROW:, :], PACK)
         y = [window_tile("y%d" % t, "y%d" % t, 2 * S if t == 0 else WINDOW) for t in range(PACK)]
-        neg_y2 = [keep.tile([P, PACK, HALF], F32, name="neg_y2_%d" % h) for h in range(2)]
+        neg_y2 = [
+            keep.tile([P, PACK, HALF], F32, name="neg_y2_a"),
+            keep.tile([P, PACK, HALF], F32, name="neg_y2_b", tag="handed_on", align_bytes=64),
+        ]
         mot = [keep.tile([P, PACK, HALF], F32, name="mot%d" % h) for h in range(2)]
 
         def gather_y2(h, t):
@@ -165,17 +168,15 @@ def tile_picked_yvideoq_mot_p_kernel(
 
         for t in range(PACK):
             gain = unit_sb[:, t : t + 1]
-            if t == 0:
+            if t < 2:
                 nc.vector.tensor_scalar(y[t][:, :S], y_banks[t][:], gain, None, MULT)
-                nc.vector.quantize_mx(out=w3_codes[:].bitcast(FP8X4), scales=w3_scale[:], in_=w3_grouped[:])
-                nc.vector.tensor_copy(neg_y2[0][:, 0, :], y[0][:].indirect(entries(t2_sb, 0, HALF)))
             else:
                 nc.scalar.activation(y[t][:, :S], y_banks[t][:], COPY, scale=gain)
+            if t > 0:
                 gather_y2(0, t)
+        nc.vector.tensor_copy(neg_y2[0][:, 0, :], y[0][:].indirect(entries(t2_sb, 0, HALF)))
+        nc.vector.quantize_mx(out=w3_codes[:].bitcast(FP8X4), scales=w3_scale[:], in_=w3_grouped[:])
 
-        ye.append(window_tile("ye3", "handed_on"))
-        nc.scalar.activation(ye[3][:, :S], ye_banks[3][:], COPY)
-        gather_eq(eq_a[:, 3 * HALF :], 3, 0, HALF)
 
         def multiply(name, mot_cols, eq_cols, width):
             hid = keep.tile([P, width * PACK], BF16, name="hid_" + name, align_bytes=64)
@@ -212,8 +213,11 @@ def tile_picked_yvideoq_mot_p_kernel(
         hid_a = multiply("a", mot[0][:], eq_a[:], HALF)
         motion(1, 0)
         answer("a", hid_a, 0, HALF, 0)
-        for t in range(1, PACK):
+        for t in range(1, PACK - 1):
             motion(1, t)
+        y1_last = keep.tile([P, HALF], F32, name="y1_last")
+        nc.scalar.activation(y1_last[:], y[3][:].indirect(entries(t1_sb, HALF, HALF)), COPY)
+        nc.vector.tensor_tensor(mot[1][:, 3, :], y1_last[:], neg_y2[1][:, 3, :], ADD)
 
         eq_b = keep.tile([P, PACK * HALF], F32, name="eq_b", tag="eq")
         waiting = None

@@ -58,9 +58,9 @@ def tile_picked_yvideoq_mot_p_kernel(
             return tile
 
         e_table = load_words("e_table", e_words, W)
-        e_bytes = load_scales("e_bytes", e_scales, W, 0)
         wrd_sb = load_list("wrd_sb", wrd)
         w2_low = load_weight("w2_low", w2[:, : H // 2])
+        e_bytes = load_scales("e_bytes", e_scales, W, 0)
         w2_high = load_weight("w2_high", w2[:, H // 2 :])
         qw_sb = load_list("qw_sb", qw)
         x_table = load_words("x_table", x_words, T)
@@ -125,7 +125,7 @@ def tile_picked_yvideoq_mot_p_kernel(
         nc.vector.tensor_copy(dealt(w2_grouped)[:, cut:], by_plane(w2_high)[:, W2_SCALAR_COLS:])
         ye_banks = first_product("w2", w2_grouped, e_picked, e_picked_bytes[:], 0)
 
-        eq_a = keep.tile([P, PACK * HALF], F32, name="eq_a", tag="eq")
+        eq_a = keep.tile([P, PACK * HALF], F32, name="eq_a")
         ye = []
 
         def gather_eq(dst, t, first, count):
@@ -134,7 +134,9 @@ def tile_picked_yvideoq_mot_p_kernel(
         for t in range(PACK):
             ye.append(window_tile("ye%d" % t, "ye%d" % t))
             nc.scalar.activation(ye[t][:, :S], ye_banks[t][:], COPY)
-            gather_eq(eq_a[:, t * HALF : (t + 1) * HALF], t, 0, HALF)
+            if t > 0:
+                gather_eq(eq_a[:, (t - 1) * HALF : t * HALF], t - 1, 0, HALF)
+        gather_eq(eq_a[:, 3 * HALF :], 3, 0, HALF)
 
         x_picked = keep.tile([P, S], U32, name="x_picked", tag="handed_on", align_bytes=64)
         x_picked_bytes = keep.tile([P, S], U8, name="x_picked_bytes", tag="w2_high", align_bytes=64)
@@ -147,13 +149,13 @@ def tile_picked_yvideoq_mot_p_kernel(
         w3_codes = keep.tile([P, N], U32, name="w3_codes", align_bytes=64)
         w3_scale = keep.tile([P, N], U8, name="w3_scale", align_bytes=64)
         nc.vector.tensor_copy(
-            w3_grouped[:].rearrange("p (c i j) -> p c j i", i=4, j=PACK),
-            w3_raw[:].rearrange("p j (c i) -> p c j i", i=4),
+            w3_grouped[:].rearrange("p (c i j) -> p c j i", i=2, j=PACK),
+            w3_raw[:].rearrange("p j (c i) -> p c j i", i=2),
         )
         y_banks = first_product("w1", w1_grouped, x_picked, x_picked_bytes[X_SCALE_ROW:, :], PACK)
         y = [window_tile("y%d" % t, "y%d" % t, 2 * S if t == 0 else WINDOW) for t in range(PACK)]
         neg_y2 = [
-            keep.tile([P, PACK, HALF], F32, name="neg_y2_a"),
+            keep.tile([P, PACK, HALF], F32, name="neg_y2_a", tag="gathered"),
             keep.tile([P, PACK, HALF], F32, name="neg_y2_b", tag="handed_on", align_bytes=64),
         ]
         mot = [keep.tile([P, PACK, HALF], F32, name="mot%d" % h) for h in range(2)]
@@ -166,24 +168,27 @@ def tile_picked_yvideoq_mot_p_kernel(
             window = y[t][:].indirect(entries(t1_sb, h * HALF, HALF))
             nc.vector.tensor_tensor(mot[h][:, t, :], window, neg_y2[h][:, t, :], op)
 
-        for t in range(PACK):
-            gain = unit_sb[:, t : t + 1]
-            if t < 2:
-                nc.vector.tensor_scalar(y[t][:, :S], y_banks[t][:], gain, None, MULT)
-            else:
-                nc.scalar.activation(y[t][:, :S], y_banks[t][:], COPY, scale=gain)
-            if t > 0:
-                gather_y2(0, t)
+        def empty_y(t):
+            nc.vector.tensor_scalar(y[t][:, :S], y_banks[t][:], unit_sb[:, t : t + 1], None, MULT)
+
+        empty_y(0)
+        empty_y(1)
         nc.vector.tensor_copy(neg_y2[0][:, 0, :], y[0][:].indirect(entries(t2_sb, 0, HALF)))
+        gather_y2(0, 1)
+        empty_y(2)
+        nc.scalar.activation(y[3][:, :S], y_banks[3][:], COPY, scale=unit_sb[:, 3:4])
+        gather_y2(0, 2)
+        motion(0, 0, SUB)
+        gather_y2(0, 3)
         nc.vector.quantize_mx(out=w3_codes[:].bitcast(FP8X4), scales=w3_scale[:], in_=w3_grouped[:])
 
 
         def multiply(name, mot_cols, eq_cols, width):
             hid = keep.tile([P, width * PACK], BF16, name="hid_" + name, align_bytes=64)
             nc.vector.tensor_tensor(
-                hid[:].rearrange("p (c i t) -> p c t i", i=4, t=PACK),
-                mot_cols.rearrange("p t (c i) -> p c t i", i=4),
-                eq_cols.rearrange("p (t c i) -> p c t i", t=PACK, i=4),
+                hid[:].rearrange("p (c i t) -> p c t i", i=2, t=PACK),
+                mot_cols.rearrange("p t (c i) -> p c t i", i=2),
+                eq_cols.rearrange("p (t c i) -> p c t i", t=PACK, i=2),
                 MULT,
             )
             return hid
@@ -206,20 +211,20 @@ def tile_picked_yvideoq_mot_p_kernel(
             nc.scalar.activation(result[:], acc[:], COPY)
             nc.sync.dma_start(out[:, first : first + width], result[:])
 
-        for t in range(PACK):
-            motion(0, t, SUB if t == 0 else ADD)
+        for t in range(1, PACK):
+            motion(0, t)
         for t in range(PACK):
             gather_y2(1, t)
-        hid_a = multiply("a", mot[0][:], eq_a[:], HALF)
-        motion(1, 0)
-        answer("a", hid_a, 0, HALF, 0)
-        for t in range(1, PACK - 1):
-            motion(1, t)
         y1_last = keep.tile([P, HALF], F32, name="y1_last")
         nc.scalar.activation(y1_last[:], y[3][:].indirect(entries(t1_sb, HALF, HALF)), COPY)
+        motion(1, 0)
+        hid_a = multiply("a", mot[0][:], eq_a[:], HALF)
+        motion(1, 1)
         nc.vector.tensor_tensor(mot[1][:, 3, :], y1_last[:], neg_y2[1][:, 3, :], ADD)
+        motion(1, 2)
+        answer("a", hid_a, 0, HALF, 0)
 
-        eq_b = keep.tile([P, PACK * HALF], F32, name="eq_b", tag="eq")
+        eq_b = keep.tile([P, PACK * HALF], F32, name="eq_b", tag="gathered")
         waiting = None
         first = 0
         for k, width in enumerate(TAIL_PIECES):

@@ -19,8 +19,10 @@ SUB = mybir.AluOpType.subtract
 
 P = 128
 PACK = 4
+LIST_ROWS = 16
 HALF = U // 2
 WINDOW = S + 16
+WIDE_WINDOW = 2 * S
 W2_SCALAR_COLS = 20
 X_SCALE_ROW = 4
 TAIL_PIECES = (256, 128, 128)
@@ -44,12 +46,12 @@ def tile_picked_yvideoq_mot_p_kernel(
             nc.sync.dma_start(tile[:].bitcast(I32), src[0].rearrange("p n t -> p (n t)").bitcast(I32))
             return tile
 
-        def load_scales(name, src, width, row):
+        def load_scales(name, src, width, first_row):
             tile = keep.tile([P, width], U8, name=name, align_bytes=64)
             nc.gpsimd.memset(tile[:].bitcast(I32), 0)
             rows = src[0].rearrange("(q r) n -> r q n", r=4)
             for r in range(4):
-                nc.sync.dma_start(tile[row + r : P : 32, :].bitcast(I32), rows[r].bitcast(I32))
+                nc.sync.dma_start(tile[first_row + r : P : 32, :].bitcast(I32), rows[r].bitcast(I32))
             return tile
 
         def load_weight(name, src):
@@ -74,8 +76,8 @@ def tile_picked_yvideoq_mot_p_kernel(
         t1_sb = load_list("t1_sb", t1)
         w3_raw = load_weight("w3_raw", w3)
 
-        def window_tile(name, tag, width=WINDOW):
-            tile = keep.tile([P, width], F32, name=name, tag=tag, align_bytes=64)
+        def window_tile(name, width):
+            tile = keep.tile([P, width], F32, name=name, tag=name, align_bytes=64)
             nc.gpsimd.memset(tile[:, S:], 0.0)
             return tile
 
@@ -110,8 +112,8 @@ def tile_picked_yvideoq_mot_p_kernel(
                 banks.append(bank)
             return banks
 
-        def entries(lst, first, count):
-            return lst[:, first // 16 : (first + count) // 16]
+        def entries(list_tile, first, count):
+            return list_tile[:, first // LIST_ROWS : (first + count) // LIST_ROWS]
 
         e_picked = keep.tile([P, S], U32, name="e_picked", align_bytes=64)
         e_picked_bytes = keep.tile([P, S], U8, name="e_picked_bytes", align_bytes=64)
@@ -132,11 +134,12 @@ def tile_picked_yvideoq_mot_p_kernel(
             nc.scalar.activation(dst, ye[t][:].indirect(entries(qw_sb, first, count)), COPY)
 
         for t in range(PACK):
-            ye.append(window_tile("ye%d" % t, "ye%d" % t))
+            ye.append(window_tile("ye%d" % t, WINDOW))
             nc.scalar.activation(ye[t][:, :S], ye_banks[t][:], COPY)
             if t > 0:
                 gather_eq(eq_a[:, (t - 1) * HALF : t * HALF], t - 1, 0, HALF)
-        gather_eq(eq_a[:, 3 * HALF :], 3, 0, HALF)
+        last = PACK - 1
+        gather_eq(eq_a[:, last * HALF :], last, 0, HALF)
 
         x_picked = keep.tile([P, S], U32, name="x_picked", tag="handed_on", align_bytes=64)
         x_picked_bytes = keep.tile([P, S], U8, name="x_picked_bytes", tag="w2_high", align_bytes=64)
@@ -153,35 +156,38 @@ def tile_picked_yvideoq_mot_p_kernel(
             w3_raw[:].rearrange("p j (c i) -> p c j i", i=2),
         )
         y_banks = first_product("w1", w1_grouped, x_picked, x_picked_bytes[X_SCALE_ROW:, :], PACK)
-        y = [window_tile("y%d" % t, "y%d" % t, 2 * S if t == 0 else WINDOW) for t in range(PACK)]
-        neg_y2 = [
-            keep.tile([P, PACK, HALF], F32, name="neg_y2_a", tag="gathered"),
-            keep.tile([P, PACK, HALF], F32, name="neg_y2_b", tag="handed_on", align_bytes=64),
+        y = [window_tile("y%d" % t, WIDE_WINDOW if t == 0 else WINDOW) for t in range(PACK)]
+
+        y2 = [
+            keep.tile([P, PACK, HALF], F32, name="y2_a", tag="gathered"),
+            keep.tile([P, PACK, HALF], F32, name="y2_b", tag="handed_on", align_bytes=64),
         ]
         mot = [keep.tile([P, PACK, HALF], F32, name="mot%d" % h) for h in range(2)]
 
-        def gather_y2(h, t):
+        def gather_negated_y2(h, t):
             window = y[t][:].indirect(entries(t2_sb, h * HALF, HALF))
-            nc.scalar.activation(neg_y2[h][:, t, :], window, COPY, scale=-1.0)
+            nc.scalar.activation(y2[h][:, t, :], window, COPY, scale=-1.0)
 
-        def motion(h, t, op=ADD):
+        def motion(h, t, op):
             window = y[t][:].indirect(entries(t1_sb, h * HALF, HALF))
-            nc.vector.tensor_tensor(mot[h][:, t, :], window, neg_y2[h][:, t, :], op)
+            nc.vector.tensor_tensor(mot[h][:, t, :], window, y2[h][:, t, :], op)
 
-        def empty_y(t):
+        def empty_y_on_vector(t):
             nc.vector.tensor_scalar(y[t][:, :S], y_banks[t][:], unit_sb[:, t : t + 1], None, MULT)
 
-        empty_y(0)
-        empty_y(1)
-        nc.vector.tensor_copy(neg_y2[0][:, 0, :], y[0][:].indirect(entries(t2_sb, 0, HALF)))
-        gather_y2(0, 1)
-        empty_y(2)
-        nc.scalar.activation(y[3][:, :S], y_banks[3][:], COPY, scale=unit_sb[:, 3:4])
-        gather_y2(0, 2)
-        motion(0, 0, SUB)
-        gather_y2(0, 3)
-        nc.vector.quantize_mx(out=w3_codes[:].bitcast(FP8X4), scales=w3_scale[:], in_=w3_grouped[:])
+        def empty_y_on_scalar(t):
+            nc.scalar.activation(y[t][:, :S], y_banks[t][:], COPY, scale=unit_sb[:, t : t + 1])
 
+        empty_y_on_vector(0)
+        empty_y_on_vector(1)
+        nc.vector.tensor_copy(y2[0][:, 0, :], y[0][:].indirect(entries(t2_sb, 0, HALF)))
+        gather_negated_y2(0, 1)
+        empty_y_on_scalar(2)
+        empty_y_on_scalar(3)
+        gather_negated_y2(0, 2)
+        motion(0, 0, SUB)
+        gather_negated_y2(0, 3)
+        nc.vector.quantize_mx(out=w3_codes[:].bitcast(FP8X4), scales=w3_scale[:], in_=w3_grouped[:])
 
         def multiply(name, mot_cols, eq_cols, width):
             hid = keep.tile([P, width * PACK], BF16, name="hid_" + name, align_bytes=64)
@@ -212,16 +218,16 @@ def tile_picked_yvideoq_mot_p_kernel(
             nc.sync.dma_start(out[:, first : first + width], result[:])
 
         for t in range(1, PACK):
-            motion(0, t)
+            motion(0, t, ADD)
         for t in range(PACK):
-            gather_y2(1, t)
+            gather_negated_y2(1, t)
         y1_last = keep.tile([P, HALF], F32, name="y1_last")
-        nc.scalar.activation(y1_last[:], y[3][:].indirect(entries(t1_sb, HALF, HALF)), COPY)
-        motion(1, 0)
+        nc.scalar.activation(y1_last[:], y[last][:].indirect(entries(t1_sb, HALF, HALF)), COPY)
+        motion(1, 0, ADD)
         hid_a = multiply("a", mot[0][:], eq_a[:], HALF)
-        motion(1, 1)
-        nc.vector.tensor_tensor(mot[1][:, 3, :], y1_last[:], neg_y2[1][:, 3, :], ADD)
-        motion(1, 2)
+        motion(1, 1, ADD)
+        nc.vector.tensor_tensor(mot[1][:, last, :], y1_last[:], y2[1][:, last, :], ADD)
+        motion(1, 2, ADD)
         answer("a", hid_a, 0, HALF, 0)
 
         eq_b = keep.tile([P, PACK * HALF], F32, name="eq_b", tag="gathered")

from contextlib import ExitStack

import concourse.mybir as mybir

K, T, S, N, H, W, U = 512, 2048, 512, 128, 512, 1024, 1024
FLOPS = 2 * (K * H * S * 2 + H * N * U)

F32 = mybir.dt.float32
BF16 = mybir.dt.bfloat16
I32 = mybir.dt.int32
U32 = mybir.dt.uint32
U16 = mybir.dt.uint16
U8 = mybir.dt.uint8
FP8X4 = mybir.dt.float8_e4m3fn_x4
COPY = mybir.ActivationFunctionType.Copy
MULT = mybir.AluOpType.mult
ADD = mybir.AluOpType.add
SUB = mybir.AluOpType.subtract

P = 128
PACK = 4
LIST_ROWS = 16
HALF = U // 2
WINDOW = S + 16
WIDE_WINDOW = 2 * S
W2_SCALAR_COLS = 20
X_SCALE_ROW = 4
TAIL_PIECES = (256, 128, 128)


def tile_picked_yvideoq_mot_p_kernel(
    tc, x_words, x_scales, w1, e_words, e_scales, w2, unit, w3, offs, wrd, t1, t2, qw, out
):
    nc = tc.nc
    with ExitStack() as ctx:
        keep = ctx.enter_context(tc.tile_pool(name="keep", bufs=1))
        psum = ctx.enter_context(tc.psum_pool(name="psum", bufs=1))

        def load_list(name, src):
            tile = keep.tile(list(src.shape), U16, name=name)
            nc.sync.dma_start(tile[:], src)
            return tile

        def load_words(name, src, width):
            tile = keep.tile([P, width], U32, name=name, align_bytes=64)
            nc.sync.dma_start(tile[:].bitcast(I32), src[0].rearrange("p n t -> p (n t)").bitcast(I32))
            return tile

        def load_scales(name, src, width, first_row):
            tile = keep.tile([P, width], U8, name=name, align_bytes=64)
            nc.gpsimd.memset(tile[:].bitcast(I32), 0)
            rows = src[0].rearrange("(q r) n -> r q n", r=4)
            for r in range(4):
                nc.sync.dma_start(tile[first_row + r : P : 32, :].bitcast(I32), rows[r].bitcast(I32))
            return tile

        def load_weight(name, src):
            tile = keep.tile([P, PACK, src.shape[1]], F32, name=name, tag=name, align_bytes=64)
            nc.sync.dma_start(tile[:], src.rearrange("(p j) c -> p j c", j=PACK))
            return tile

        e_table = load_words("e_table", e_words, W)
        wrd_sb = load_list("wrd_sb", wrd)
        w2_low = load_weight("w2_low", w2[:, : H // 2])
        e_bytes = load_scales("e_bytes", e_scales, W, 0)
        w2_high = load_weight("w2_high", w2[:, H // 2 :])
        qw_sb = load_list("qw_sb", qw)
        x_table = load_words("x_table", x_words, T)
        offs_sb = load_list("offs_sb", offs)
        x_bytes = load_scales("x_bytes", x_scales, T, X_SCALE_ROW)
        w1_low = load_weight("w1_low", w1[:, : H // 2])
        w1_high = load_weight("w1_high", w1[:, H // 2 :])
        unit_sb = keep.tile([P, PACK], F32, name="unit_sb")
        nc.sync.dma_start(unit_sb[:], unit.rearrange("(p t) o -> p (t o)", t=PACK))
        t2_sb = load_list("t2_sb", t2)
        t1_sb = load_list("t1_sb", t1)
        w3_raw = load_weight("w3_raw", w3)

        def window_tile(name, width):
            tile = keep.tile([P, width], F32, name=name, tag=name, align_bytes=64)
            nc.gpsimd.memset(tile[:, S:], 0.0)
            return tile

        def dealt(grouped):
            return grouped[:].rearrange("p (t m j) -> p m j t", t=PACK, j=PACK)

        def by_plane(raw):
            return raw[:].rearrange("p j (m t) -> p m j t", t=PACK)

        def first_product(name, grouped, picked_words, picked_bytes, first_bank):
            codes = keep.tile([P, H], U32, name=name + "_codes", align_bytes=64)
            scales = keep.tile([P, H], U8, name=name + "_scales", align_bytes=64)
            for lo, hi in ((0, P), (P, H)):
                nc.vector.quantize_mx(
                    out=codes[:, lo:hi].bitcast(FP8X4),
                    scales=scales[:, lo:hi],
                    in_=grouped[:, PACK * lo : PACK * hi],
                )
            banks = []
            for t in range(PACK):
                cols = slice(t * P, (t + 1) * P)
                bank = psum.tile([P, S], F32, name=name + "_acc%d" % t, tag="bank%d" % (first_bank + t))
                nc.tensor.matmul_mx(
                    out=bank[:],
                    lhsT=codes[:, cols].bitcast(FP8X4),
                    lhsT_scale=scales[:, cols],
                    rhs=picked_words[:].bitcast(FP8X4),
                    rhs_scale=picked_bytes,
                    start=True,
                    stop=True,
                )
                banks.append(bank)
            return banks

        def entries(list_tile, first, count):
            return list_tile[:, first // LIST_ROWS : (first + count) // LIST_ROWS]

        e_picked = keep.tile([P, S], U32, name="e_picked", align_bytes=64)
        e_picked_bytes = keep.tile([P, S], U8, name="e_picked_bytes", align_bytes=64)
        w2_grouped = keep.tile([P, PACK * H], BF16, name="w2_grouped", tag="handed_on", align_bytes=64)
        nc.vector.tensor_copy(e_picked[:], e_table[:].indirect(wrd_sb[:]))
        nc.vector.tensor_copy(e_picked_bytes[:], e_bytes[:].indirect(wrd_sb[:]))
        mid = P // 2
        cut = mid + W2_SCALAR_COLS
        nc.scalar.activation(dealt(w2_grouped)[:, :mid], by_plane(w2_low), COPY)
        nc.scalar.activation(dealt(w2_grouped)[:, mid:cut], by_plane(w2_high)[:, :W2_SCALAR_COLS], COPY)
        nc.vector.tensor_copy(dealt(w2_grouped)[:, cut:], by_plane(w2_high)[:, W2_SCALAR_COLS:])
        ye_banks = first_product("w2", w2_grouped, e_picked, e_picked_bytes[:], 0)

        eq_a = keep.tile([P, PACK * HALF], F32, name="eq_a")
        ye = []

        def gather_eq(dst, t, first, count):
            nc.scalar.activation(dst, ye[t][:].indirect(entries(qw_sb, first, count)), COPY)

        for t in range(PACK):
            ye.append(window_tile("ye%d" % t, WINDOW))
            nc.scalar.activation(ye[t][:, :S], ye_banks[t][:], COPY)
            if t > 0:
                gather_eq(eq_a[:, (t - 1) * HALF : t * HALF], t - 1, 0, HALF)
        last = PACK - 1
        gather_eq(eq_a[:, last * HALF :], last, 0, HALF)

        x_picked = keep.tile([P, S], U32, name="x_picked", tag="handed_on", align_bytes=64)
        x_picked_bytes = keep.tile([P, S], U8, name="x_picked_bytes", tag="w2_high", align_bytes=64)
        w1_grouped = keep.tile([P, PACK * H], BF16, name="w1_grouped", align_bytes=64)
        nc.vector.tensor_copy(x_picked[:], x_table[:].indirect(offs_sb[:]))
        nc.vector.tensor_copy(x_picked_bytes[:], x_bytes[:].indirect(offs_sb[:]))
        nc.vector.tensor_copy(dealt(w1_grouped)[:, :mid], by_plane(w1_low))
        nc.vector.tensor_copy(dealt(w1_grouped)[:, mid:], by_plane(w1_high))
        w3_grouped = keep.tile([P, PACK * N], BF16, name="w3_grouped", align_bytes=64)
        w3_codes = keep.tile([P, N], U32, name="w3_codes", align_bytes=64)
        w3_scale = keep.tile([P, N], U8, name="w3_scale", align_bytes=64)
        nc.vector.tensor_copy(
            w3_grouped[:].rearrange("p (c i j) -> p c j i", i=2, j=PACK),
            w3_raw[:].rearrange("p j (c i) -> p c j i", i=2),
        )
        y_banks = first_product("w1", w1_grouped, x_picked, x_picked_bytes[X_SCALE_ROW:, :], PACK)
        y = [window_tile("y%d" % t, WIDE_WINDOW if t == 0 else WINDOW) for t in range(PACK)]

        y2 = [
            keep.tile([P, PACK, HALF], F32, name="y2_a", tag="gathered"),
            keep.tile([P, PACK, HALF], F32, name="y2_b", tag="handed_on", align_bytes=64),
        ]
        mot = [keep.tile([P, PACK, HALF], F32, name="mot%d" % h) for h in range(2)]

        def gather_negated_y2(h, t):
            window = y[t][:].indirect(entries(t2_sb, h * HALF, HALF))
            nc.scalar.activation(y2[h][:, t, :], window, COPY, scale=-1.0)

        def motion(h, t, op):
            window = y[t][:].indirect(entries(t1_sb, h * HALF, HALF))
            nc.vector.tensor_tensor(mot[h][:, t, :], window, y2[h][:, t, :], op)

        def empty_y_on_vector(t):
            nc.vector.tensor_scalar(y[t][:, :S], y_banks[t][:], unit_sb[:, t : t + 1], None, MULT)

        def empty_y_on_scalar(t):
            nc.scalar.activation(y[t][:, :S], y_banks[t][:], COPY, scale=unit_sb[:, t : t + 1])

        empty_y_on_vector(0)
        empty_y_on_vector(1)
        nc.vector.tensor_copy(y2[0][:, 0, :], y[0][:].indirect(entries(t2_sb, 0, HALF)))
        gather_negated_y2(0, 1)
        empty_y_on_scalar(2)
        empty_y_on_scalar(3)
        gather_negated_y2(0, 2)
        motion(0, 0, SUB)
        gather_negated_y2(0, 3)
        nc.vector.quantize_mx(out=w3_codes[:].bitcast(FP8X4), scales=w3_scale[:], in_=w3_grouped[:])

        def multiply(name, mot_cols, eq_cols, width):
            hid = keep.tile([P, width * PACK], BF16, name="hid_" + name, align_bytes=64)
            nc.vector.tensor_tensor(
                hid[:].rearrange("p (c i t) -> p c t i", i=2, t=PACK),
                mot_cols.rearrange("p t (c i) -> p c t i", i=2),
                eq_cols.rearrange("p (t c i) -> p c t i", t=PACK, i=2),
                MULT,
            )
            return hid

        def answer(name, hid, first, width, bank):
            codes = keep.tile([P, width], U32, name="hid_codes_" + name, align_bytes=64)
            scales = keep.tile([P, width], U8, name="hid_scales_" + name, align_bytes=64)
            nc.vector.quantize_mx(out=codes[:].bitcast(FP8X4), scales=scales[:], in_=hid[:])
            acc = psum.tile([P, width], F32, name="acc_" + name, tag="bank%d" % bank)
            nc.tensor.matmul_mx(
                out=acc[:],
                lhsT=w3_codes[:].bitcast(FP8X4),
                lhsT_scale=w3_scale[:],
                rhs=codes[:].bitcast(FP8X4),
                rhs_scale=scales[:],
                start=True,
                stop=True,
            )
            result = keep.tile([P, width], F32, name="result_" + name)
            nc.scalar.activation(result[:], acc[:], COPY)
            nc.sync.dma_start(out[:, first : first + width], result[:])

        for t in range(1, PACK):
            motion(0, t, ADD)
        for t in range(PACK):
            gather_negated_y2(1, t)
        y1_last = keep.tile([P, HALF], F32, name="y1_last")
        nc.scalar.activation(y1_last[:], y[last][:].indirect(entries(t1_sb, HALF, HALF)), COPY)
        motion(1, 0, ADD)
        hid_a = multiply("a", mot[0][:], eq_a[:], HALF)
        motion(1, 1, ADD)
        nc.vector.tensor_tensor(mot[1][:, last, :], y1_last[:], y2[1][:, last, :], ADD)
        motion(1, 2, ADD)
        answer("a", hid_a, 0, HALF, 0)

        eq_b = keep.tile([P, PACK * HALF], F32, name="eq_b", tag="gathered")
        waiting = None
        first = 0
        for k, width in enumerate(TAIL_PIECES):
            piece = eq_b[:, PACK * first : PACK * (first + width)]
            for t in range(PACK):
                gather_eq(piece[:, t * width : (t + 1) * width], t, HALF + first, width)
            hid = multiply("b%d" % k, mot[1][:, :, first : first + width], piece, width)
            if waiting:
                answer(*waiting)
            waiting = ("b%d" % k, hid, HALF + first, width, 1 + k)
            first = first + width
        answer(*waiting)
